import numpy as np
import ml_dtypes


def mxq(x, axis, fmt="e4m3"):
    dtype, down = {"e4m3": (ml_dtypes.float8_e4m3fn, 7), "e5m2": (ml_dtypes.float8_e5m2, 14)}[fmt]
    v = np.moveaxis(np.asarray(x, np.float32).astype(ml_dtypes.bfloat16).astype(np.float64), axis, -1)
    blocks = v.reshape(v.shape[:-1] + (-1, 32))
    amax = np.abs(blocks).max(-1, keepdims=True)
    byte = np.maximum(np.where(amax > 0, np.frexp(amax)[1] - 1 + 127, 0) - down, 1)
    scale = np.exp2(byte - 127.0)
    codes = (blocks / scale).astype(np.float32).astype(dtype).astype(np.float64)
    return np.moveaxis((codes * scale).reshape(v.shape), -1, axis)


WIDE = False


def mx_kscale(k, group=512):
    if not WIDE:
        return np.ones(k)
    levels = np.array([18, -18])
    if group != 512:
        return np.exp2(np.random.permutation(np.resize(levels, k // group))).repeat(group)
    if k % 512:
        return np.exp2(np.random.permutation(np.resize(levels, k // 32))).repeat(32)
    a = np.empty((k // 512, 16))
    for p in range(k // 512):
        a[p, :8] = np.random.permutation(np.resize(levels, 8))
        for g in range(8):
            far = levels[np.abs(levels - a[p, g]) >= 10]
            a[p, g + 8] = far[np.random.randint(len(far))]
    return np.exp2(a.ravel()).repeat(32)


def f64(x):
    return np.asarray(x).astype(np.float64)


def gelu(v):
    return 0.5 * v * (1.0 + np.tanh(0.7978845608028654 * (v + 0.044715 * v ** 3)))


G, D, K, M, N = 4, 128, 1024, 128, 512


def setup_inputs():
    n = np.random.standard_normal
    s = mx_kscale(D, 0)[:, None]
    u = mx_kscale(K)[:, None]
    return {
        "x": (n((G, D, N)) * s).astype(np.float32),
        "w1": (n((G, D, K)) / np.sqrt(D) / s).astype(np.float32),
        "hs": (np.random.uniform(0.5, 2.0, (G, K, 1)) * u).astype(np.float32),
        "w2": (n((G, K, M)) / np.sqrt(K) / u).astype(np.float32),
        "b": (0.5 * n((G, K, 1))).astype(np.float32),
    }


def reference(x, w1, hs, w2, b):
    xq = mxq(f64(x), 1, "e4m3")
    h = mxq(f64(w1), 1, "e4m3").transpose(0, 2, 1) @ xq
    h = h + f64(b)
    h = (gelu(h)) * f64(hs)
    y = mxq(f64(w2), 1, "e4m3").transpose(0, 2, 1) @ mxq(h, 1, "e4m3")
    return y

from contextlib import ExitStack

import concourse.mybir as mybir

G, D, K, M, N = 4, 128, 1024, 128, 512
FLOPS = 2 * G * N * K * (D + M)

F32 = mybir.dt.float32
BF16 = mybir.dt.bfloat16
U32 = mybir.dt.uint32
U8 = mybir.dt.uint8
FP8X4 = mybir.dt.float8_e4m3fn_x4
GELU = mybir.ActivationFunctionType.Gelu_apprx_tanh
MULT = mybir.AluOpType.mult

P = 128
PACK = 4
ROWS = D // PACK
K_PASS = P * PACK
PASSES = K // K_PASS
N_MM = 512
BANK = 512

BANKS = [2, 2, 1, 2]
LOADS = [('x', 0, 512), ('w1', 0, 512), ('b', 0), ('w1', 512, 1024), ('hs', 0), ('w2', 0), ('b', 1), ('w2', 1), ('hs', 1), ('w2', 2), ('w2', 3)]
ORDER = [
    ('cast_x', 'S', 352, 512),
    ('cast_x', 'V', 0, 352),
    ('quant_x', 'V', 0, 512),
    ('cast_w1', 'S', 0, 0, 128, 1, 2),
    ('cast_w1', 'V', 0, 0, 128, 0, 1),
    ('quant_w1', 'V', 0, 0, 1),
    ('quant_w1', 'V', 0, 1, 2),
    ('z', 'P', 0, 0, 0, 512, 0),
    ('quant_w1', 'V', 0, 2, 4),
    ('z', 'P', 0, 0, 0, 512, 2),
    ('gelu', 'S', 0, 0, 0, 512, 0),
    ('z', 'P', 1, 0, 0, 512, 3),
    ('cast_w1', 'V', 1, 0, 128, 0, 1),
    ('gelu', 'S', 0, 0, 0, 512, 2),
    ('z', 'P', 0, 0, 0, 512, 1),
    ('gelu', 'S', 1, 0, 0, 512, 3),
    ('cast_w1', 'V', 1, 0, 128, 1, 2),
    ('z', 'P', 0, 0, 0, 512, 3),
    ('gelu', 'S', 0, 0, 0, 512, 1),
    ('z', 'P', 1, 0, 0, 512, 2),
    ('cast_w2', 'V', 0, 0),
    ('z', 'P', 1, 0, 0, 512, 1),
    ('gelu', 'S', 0, 0, 0, 512, 3),
    ('quant_w1', 'V', 1, 0, 4),
    ('z', 'P', 2, 0, 0, 512, 0),
    ('gelu', 'S', 1, 0, 0, 512, 2),
    ('cast_w2', 'V', 0, 1),
    ('z', 'P', 0, 1, 0, 512, 1),
    ('scale', 'V', 0, 0, 0, 512),
    ('gelu', 'S', 2, 0, 0, 512, 0),
    ('z', 'P', 1, 0, 0, 512, 0),
    ('gelu', 'S', 1, 0, 0, 512, 1),
    ('z', 'P', 0, 1, 0, 512, 0),
    ('z', 'P', 2, 0, 0, 512, 3),
    ('gelu', 'S', 1, 0, 0, 512, 0),
    ('gelu', 'S', 0, 1, 0, 512, 1),
    ('scale', 'V', 1, 0, 0, 512),
    ('gelu', 'S', 2, 0, 0, 512, 3),
    ('z', 'P', 0, 1, 0, 512, 3),
    ('gelu', 'S', 0, 1, 0, 512, 0),
    ('z', 'P', 2, 0, 0, 512, 1),
    ('gelu', 'S', 0, 1, 0, 512, 3),
    ('z', 'P', 0, 1, 0, 512, 2),
    ('gelu', 'S', 2, 0, 0, 512, 1),
    ('z', 'P', 3, 0, 0, 512, 1),
    ('quant_w2', 'V', 0),
    ('quant_h', 'V', 1, 0, 0, 512),
    ('z', 'P', 1, 1, 0, 512, 3),
    ('gelu', 'S', 0, 1, 0, 512, 2),
    ('quant_h', 'V', 0, 0, 0, 512),
    ('z', 'P', 2, 0, 0, 512, 2),
    ('gelu', 'S', 3, 0, 0, 512, 1),
    ('z', 'P', 3, 0, 0, 512, 0),
    ('scale', 'V', 0, 1, 0, 512),
    ('gelu', 'S', 2, 0, 0, 512, 2),
    ('z', 'P', 1, 1, 0, 512, 1),
    ('gelu', 'S', 1, 1, 0, 512, 3),
    ('z', 'P', 3, 0, 0, 512, 2),
    ('z', 'P', 2, 1, 0, 512, 1),
    ('gelu', 'S', 1, 1, 0, 512, 1),
    ('z', 'P', 1, 1, 0, 512, 2),
    ('gelu', 'S', 3, 0, 0, 512, 0),
    ('scale', 'V', 2, 0, 0, 512),
    ('y', 'P', 0, 0, 512, 0),
    ('gelu', 'S', 3, 0, 0, 512, 2),
    ('z', 'P', 3, 0, 0, 512, 3),
    ('gelu', 'S', 1, 1, 0, 512, 2),
    ('z', 'P', 1, 1, 0, 512, 0),
    ('gelu', 'S', 2, 1, 0, 512, 1),
    ('gelu', 'S', 1, 1, 0, 512, 0),
    ('z', 'P', 2, 1, 0, 512, 0),
    ('quant_h', 'V', 0, 1, 0, 512),
    ('gelu', 'S', 3, 0, 0, 512, 3),
    ('quant_h', 'V', 2, 0, 0, 512),
    ('y', 'P', 0, 0, 512, 1),
    ('gelu', 'S', 2, 1, 0, 512, 0),
    ('scale', 'V', 3, 0, 0, 512),
    ('cast_w2', 'S', 2, 1),
    ('z', 'P', 2, 1, 0, 512, 2),
    ('cast_w2', 'S', 2, 0),
    ('gelu', 'S', 2, 1, 0, 512, 2),
    ('scale', 'V', 1, 1, 0, 512),
    ('cast_w2', 'S', 1, 0),
    ('z', 'P', 2, 1, 0, 512, 3),
    ('z', 'P', 3, 1, 0, 512, 1),
    ('cast_w2', 'S', 1, 1),
    ('z', 'P', 3, 1, 0, 512, 0),
    ('gelu', 'S', 2, 1, 0, 512, 3),
    ('gelu', 'S', 3, 1, 0, 512, 1),
    ('scale', 'V', 2, 1, 0, 512),
    ('cast_w2', 'S', 3, 1),
    ('z', 'P', 3, 1, 0, 512, 2),
    ('gelu', 'S', 3, 1, 0, 512, 0),
    ('out', 'S', 0, 0, 512),
    ('z', 'P', 3, 1, 0, 512, 3),
    ('gelu', 'S', 3, 1, 0, 512, 2),
    ('quant_w2', 'V', 1),
    ('quant_w2', 'V', 2),
    ('y', 'P', 1, 0, 512, 0),
    ('cast_w2', 'S', 3, 0),
    ('quant_h', 'V', 1, 1, 0, 512),
    ('gelu', 'S', 3, 1, 0, 512, 3),
    ('quant_h', 'V', 2, 1, 0, 512),
    ('y', 'P', 1, 0, 512, 1),
    ('warm', 'P'),
    ('warm', 'P'),
    ('quant_h', 'V', 3, 0, 0, 512),
    ('out', 'S', 1, 0, 512),
    ('scale', 'V', 3, 1, 0, 512),
    ('y', 'P', 2, 0, 512, 0),
    ('y', 'P', 2, 0, 512, 1),
    ('warm', 'P'),
    ('warm', 'P'),
    ('out', 'S', 2, 0, 512),
    ('quant_w2', 'V', 3),
    ('quant_h', 'V', 3, 1, 0, 512),
    ('y', 'P', 3, 0, 512, 0),
    ('y', 'P', 3, 0, 512, 1),
    ('out', 'V', 3, 0, 384),
    ('out', 'S', 3, 384, 512),
]


def tile_rows_gmlp_gelu_bias_kernel(tc, x, w1, hs, w2, b, out):
    nc = tc.nc
    with ExitStack() as ctx:
        sb = ctx.enter_context(tc.tile_pool(name="sb", bufs=1))
        ps = ctx.enter_context(tc.psum_pool(name="ps", bufs=1))
        ctx.enter_context(tc.manual_schedule())

        x_hbm = x.rearrange("g (p j) n -> (g p) j n", j=PACK)
        w1_hbm = w1.rearrange("g (p j) k -> (g p) j k", j=PACK)

        warm_in = sb.tile([P, 8], F32, name="warm_in")
        warm_out = sb.tile([P, 8], F32, name="warm_out")
        nc.gpsimd.memset(warm_in[:], 0.0)
        nc.scalar.activation(out=warm_out[:], in_=warm_in[:], func=GELU)

        raw = {}
        for load in LOADS:
            name = "raw_" + "_".join(map(str, load))
            if load[0] == "x" or load[0] == "w1":
                src = x_hbm if load[0] == "x" else w1_hbm
                raw[load] = sb.tile([P, PACK, load[2] - load[1]], F32, name=name)
                nc.sync.dma_start(out=raw[load][:], in_=src[:, :, load[1] : load[2]])
            elif load[0] == "w2":
                raw[load] = sb.tile([P, PASSES, PACK * M], F32, name=name)
                nc.sync.dma_start(out=raw[load][:], in_=w2[load[1]].rearrange("(a p j) m -> p a (j m)", p=P, j=PACK))
            else:
                src = b if load[0] == "b" else hs
                raw[load] = sb.tile([P, G, 8], F32, name=name)
                nc.sync.dma_start(
                    out=raw[load][:, :, 0:PACK],
                    in_=src.rearrange("g (a p r) o -> a p g (r o)", p=P, r=PACK)[load[1]],
                )

        def mx_tiles(name, width):
            grouped = sb.tile([P, width * PACK], BF16, name=name + "_bf16", align_bytes=64)
            codes = sb.tile([P, width], U32, name=name + "_codes", align_bytes=64)
            scales = sb.tile([P, width], U8, name=name + "_scales", align_bytes=64)
            return grouped, codes, scales

        x_mx = mx_tiles("x", N)
        w1_mx = [mx_tiles("w1_%d" % a, K_PASS) for a in range(PASSES)]
        w2_mx = [mx_tiles("w2_%d" % g, PASSES * M) for g in range(G)]
        h_mx = {(g, a): mx_tiles("h_%d_%d" % (g, a), N) for g in range(G) for a in range(PASSES)}

        z_banks = [[ps.tile([P, BANK], F32, name="z_%d_%d" % (g, i)) for i in range(BANKS[g])] for g in range(G)]
        y_bank = ps.tile([P, BANK], F32, name="y")
        fills = [0] * G
        bank_of = {}
        act = {}

        def copy_on(engine, dst, src):
            if engine == "S":
                nc.scalar.copy(out=dst, in_=src)
            else:
                nc.vector.tensor_copy(out=dst, in_=src)

        def find(kind, c0):
            return [l for l in LOADS if l[0] == kind and l[1] <= c0 < l[2]][0]

        def interleave(engine, grouped, c0, width, src):
            dst = grouped[:, PACK * c0 : PACK * (c0 + width)].rearrange("p (c i j) -> p c j i", i=2, j=PACK)
            copy_on(engine, dst, src.rearrange("p j (c i) -> p c j i", i=2))

        def quantize(mx, c0, c1):
            grouped, codes, scales = mx
            nc.vector.quantize_mx(
                out=codes[:, c0:c1].bitcast(FP8X4), scales=scales[:, c0:c1], in_=grouped[:, PACK * c0 : PACK * c1]
            )

        def slots(n0, n1, r0):
            width = n1 - n0
            per = BANK // width
            return [(r, (r - r0) * width) for r in range(r0, min(PACK, r0 + per))]

        for step in ORDER:
            kind, engine = step[0], step[1]
            if kind == "cast_x":
                n0, n1 = step[2:]
                load = find("x", n0)
                interleave(engine, x_mx[0], n0, n1 - n0, raw[load][:, :, n0 - load[1] : n1 - load[1]])
            elif kind == "cast_w2":
                g, a = step[2:]
                src = raw[("w2", g)][:, a, :].rearrange("p (j m) -> p j m", j=PACK)
                interleave(engine, w2_mx[g][0], a * M, M, src)
            elif kind == "cast_w1":
                a, s0, s1, u0, u1 = step[2:]
                load = find("w1", a * K_PASS + PACK * s0)
                k0 = a * K_PASS - load[1]
                src = raw[load][:, :, k0 + PACK * s0 : k0 + PACK * s1].rearrange("p j (s u i) -> p u s j i", u=2, i=2)
                dst = w1_mx[a][0][:].rearrange("p (u i s j) -> p u s j i", u=2, i=2, j=PACK)[:, :, s0:s1, :, :]
                if u1 - u0 == 1:
                    copy_on(engine, dst[:, u0], src[:, u0])
                else:
                    copy_on(engine, dst, src)
            elif kind == "quant_x":
                quantize(x_mx, step[2], step[3])
            elif kind == "quant_w1":
                quantize(w1_mx[step[2]], P * step[3], P * step[4])
            elif kind == "quant_w2":
                quantize(w2_mx[step[2]], 0, PASSES * M)
            elif kind == "quant_h":
                g, a, n0, n1 = step[2:]
                quantize(h_mx[g, a], n0, n1)
            elif kind == "z":
                g, a, n0, n1, r0 = step[2:]
                bank = z_banks[g][fills[g] % BANKS[g]]
                fills[g] += 1
                bank_of[step[2:]] = bank
                rows = slice(ROWS * g, ROWS * (g + 1))
                for r, at in slots(n0, n1, r0):
                    cols = slice(P * r, P * (r + 1))
                    for c in range(0, n1 - n0, N_MM):
                        nc.tensor.matmul_mx(
                            out=bank[:, at + c : at + c + N_MM],
                            lhsT=w1_mx[a][1][rows, cols].bitcast(FP8X4),
                            lhsT_scale=w1_mx[a][2][rows, cols],
                            rhs=x_mx[1][rows, n0 + c : n0 + c + N_MM].bitcast(FP8X4),
                            rhs_scale=x_mx[2][rows, n0 + c : n0 + c + N_MM],
                            start=True,
                            stop=True,
                        )
            elif kind == "warm":
                for g in range(G):
                    rows = slice(ROWS * g, ROWS * (g + 1))
                    nc.tensor.matmul_mx(
                        out=z_banks[g][fills[g] % BANKS[g]][:],
                        lhsT=w1_mx[1][1][rows, 0:P].bitcast(FP8X4),
                        lhsT_scale=w1_mx[1][2][rows, 0:P],
                        rhs=x_mx[1][rows, :].bitcast(FP8X4),
                        rhs_scale=x_mx[2][rows, :],
                        start=True,
                        stop=True,
                    )
            elif kind == "gelu":
                g, a, n0, n1, r0 = step[2:]
                key = (g, a, n0, n1)
                if key not in act:
                    act[key] = sb.tile([P, PACK, n1 - n0], F32, name="act_%d_%d_%d_%d" % key)
                bank = bank_of[step[2:]]
                for r, at in slots(n0, n1, r0):
                    nc.scalar.activation(
                        out=act[key][:, r, :],
                        in_=bank[:, at : at + n1 - n0],
                        func=GELU,
                        bias=raw["b", a][:, g, r : r + 1],
                    )
            elif kind == "scale":
                g, a, n0, n1 = step[2:]
                pairs = (n1 - n0) // 2
                nc.vector.tensor_tensor(
                    out=h_mx[g, a][0][:, PACK * n0 : PACK * n1].rearrange("p (c i r) -> p c r i", i=2, r=PACK),
                    in0=act[g, a, n0, n1][:].rearrange("p r (c i) -> p c r i", i=2),
                    in1=raw["hs", a][:, g, 0:PACK].unsqueeze(1).unsqueeze(3).to_broadcast([P, pairs, PACK, 2]),
                    op=MULT,
                )
            elif kind == "y":
                g, n0, n1 = step[2:5]
                for c in range(n0, n1, N_MM):
                    for a in step[5:] or range(PASSES):
                        nc.tensor.matmul_mx(
                            out=y_bank[:, c : c + N_MM],
                            lhsT=w2_mx[g][1][:, M * a : M * (a + 1)].bitcast(FP8X4),
                            lhsT_scale=w2_mx[g][2][:, M * a : M * (a + 1)],
                            rhs=h_mx[g, a][1][:, c : c + N_MM].bitcast(FP8X4),
                            rhs_scale=h_mx[g, a][2][:, c : c + N_MM],
                            start=(a == 0),
                            stop=(a == PASSES - 1),
                        )
            else:
                g, n0, n1 = step[2:]
                y_sb = sb.tile([P, n1 - n0], F32, name="y_%d_%d" % (g, n0))
                copy_on(engine, y_sb[:], y_bank[:, n0:n1])
                nc.sync.dma_start(out=out[g, :, n0:n1], in_=y_sb[:])
